import numpy as np
import ml_dtypes


def mxq(x, axis, fmt="e4m3"):
    dtype, down = {"e4m3": (ml_dtypes.float8_e4m3fn, 7), "e5m2": (ml_dtypes.float8_e5m2, 14)}[fmt]
    v = np.moveaxis(np.asarray(x, np.float32).astype(ml_dtypes.bfloat16).astype(np.float64), axis, -1)
    blocks = v.reshape(v.shape[:-1] + (-1, 32))
    amax = np.abs(blocks).max(-1, keepdims=True)
    byte = np.maximum(np.where(amax > 0, np.frexp(amax)[1] - 1 + 127, 0) - down, 1)
    scale = np.exp2(byte - 127.0)
    codes = (blocks / scale).astype(np.float32).astype(dtype).astype(np.float64)
    return np.moveaxis((codes * scale).reshape(v.shape), -1, axis)


WIDE = False


def mx_kscale(k):
    if not WIDE:
        return np.ones(k)
    levels = np.array([10, -10, 5, -5, 0])
    if k % 512:
        return np.exp2(np.random.permutation(np.resize(levels, k // 32))).repeat(32)
    a = np.empty((k // 512, 16))
    for p in range(k // 512):
        a[p, :8] = np.random.permutation(np.resize(levels, 8))
        for g in range(8):
            far = levels[np.abs(levels - a[p, g]) >= 10]
            a[p, g + 8] = far[np.random.randint(len(far))]
    return np.exp2(a.ravel()).repeat(32)


def f64(x):
    return np.asarray(x).astype(np.float64)


def striped(idx):
    return np.tile(np.asarray(idx).reshape(-1, 16).T, (8, 1)).astype(np.uint16)


def unstriped(offs):
    return offs[:16].T.reshape(-1).astype(np.int64)


def striped8(idx):
    return np.asarray(idx).reshape(8, -1, 16).transpose(0, 2, 1).reshape(128, -1).astype(np.uint16)


def unstriped8(offs):
    return offs.reshape(8, 16, -1).transpose(0, 2, 1).reshape(8, -1).astype(np.int64)


def pick8(x, idx, run):
    r = np.arange(len(x))
    return x[r[:, None], idx[r % (8 * run) // run]]


E2M1 = np.array([0.0, 0.5, 1.0, 1.5, 2.0, 3.0, 4.0, 6.0, -0.0, -0.5, -1.0, -1.5, -2.0, -3.0, -4.0, -6.0])


def pack_weight(w, fmt):
    k, n = w.shape
    w = f64(np.asarray(w, np.float32).astype(ml_dtypes.bfloat16)).reshape(k // 32, 32, n)
    amax = np.abs(w).max(1)
    if fmt == "e4m3":
        byte = np.frexp(amax)[1] - 1 + 127 - 7
    else:
        mant, ex = np.frexp(amax / 6.0)
        byte = np.where(mant > 0.5, ex, ex - 1) + 127
    byte = np.clip(np.where(amax > 0, byte, 1), 1, 254)
    scaled = (w * np.exp2(127.0 - byte)[:, None, :]).reshape(k, n).astype(np.float32)
    by_word = np.ascontiguousarray(scaled.reshape(k // 512, 128, 4, n).transpose(0, 1, 3, 2))
    if fmt == "e4m3":
        words = by_word.astype(ml_dtypes.float8_e4m3fn).view(np.uint8)
    else:
        c = by_word.astype(ml_dtypes.float4_e2m1fn).view(np.uint8) & 0xF
        words = (c[..., 0::2] | (c[..., 1::2] << 4)).reshape(k // 512, 128, 2 * n)
    return np.ascontiguousarray(words), np.ascontiguousarray(byte.astype(np.uint8).reshape(k // 512, 16, n))


def unpack_weight(words, scales, fmt):
    g, _, n = scales.shape
    words = np.ascontiguousarray(words).reshape(g, 128, n, -1)
    if fmt == "e4m3":
        vals = words.view(ml_dtypes.float8_e4m3fn).astype(np.float64)
    else:
        nib = np.empty((g, 128, n, 4), np.uint8)
        nib[..., 0::2] = words & 0xF
        nib[..., 1::2] = words >> 4
        vals = E2M1[nib]
    vals = vals * np.repeat(np.exp2(scales.astype(np.float64) - 127.0), 8, axis=1)[..., None]
    return vals.transpose(0, 1, 3, 2).reshape(g * 512, n)


def sigmoid(v):
    return 1.0 / (1.0 + np.exp(-v))


K, R, F, T, J, M = 512, 128, 512, 2048, 512, 256


def setup_inputs():
    n = np.random.standard_normal
    idx = np.random.permutation(T)[:J]
    idx2 = np.stack([np.random.permutation(J)[:M] for _ in range(8)])
    idx3 = np.stack([np.random.permutation(J)[:M] for _ in range(8)])
    fk = mx_kscale(K)
    ff = mx_kscale(F)
    tabp = pack_weight(n((K, T)) / fk[:, None], "e4m3")
    return {
        "tab_words": tabp[0],
        "tab_scales": tabp[1],
        "w1": (n((K, R)) * 1 / np.sqrt(K) * fk[:, None]).astype(np.float32),
        "gain": (np.random.uniform(0.5, 1.5, (R, 1))).astype(np.float32),
        "steep": (np.random.uniform(0.7, 2.5, (R, 1))).astype(np.float32),
        "wo": (n((F, R)) * 1 / np.sqrt(F) * ff[:, None]).astype(np.float32),
        "dy": (n((F, M)) / ff[:, None]).astype(np.float32),
        "og": (np.random.uniform(0.3, 1.0, (R, 1))).astype(np.float32),
        "base": (0.3 * n((R, J))).astype(np.float32),
        "offs": striped(idx),
        "offs2": striped8(idx2),
        "offs3": striped8(idx3),
    }


def reference(tab_words, tab_scales, w1, gain, steep, wo, dy, og, base, offs, offs2, offs3):
    idx = unstriped(offs)
    idx2 = unstriped8(offs2)
    idx3 = unstriped8(offs3)
    tabu = unpack_weight(tab_words, tab_scales, "e4m3")
    w1q = mxq(f64(w1), 0, "e4m3")
    tabidxg = tabu[:, idx]
    a = w1q.T @ tabidxg
    h1 = a * f64(gain)
    gt = sigmoid((pick8(h1, idx2, 16) - pick8(h1, idx3, 16)) * f64(steep))
    woq = mxq(f64(wo), 0, "e4m3")
    dyq = mxq(f64(dy), 0, "e4m3")
    c0 = woq.T @ dyq
    dgt = c0 * (pick8(h1, idx2, 16) - pick8(h1, idx3, 16))
    s1 = np.zeros((R, J))
    s1[np.arange(R)[:, None], idx3[np.arange(R) % 128 // 16]] = c0
    e2 = c0 * gt * (-1.0)
    s2 = np.zeros((R, J))
    s2[np.arange(R)[:, None], idx3[np.arange(R) % 128 // 16]] = e2
    e3 = dgt * gt * (1.0 - gt) * f64(steep) * (-1.0)
    s3 = np.zeros((R, J))
    s3[np.arange(R)[:, None], idx3[np.arange(R) % 128 // 16]] = e3
    e4 = c0 * gt
    s4 = np.zeros((R, J))
    s4[np.arange(R)[:, None], idx2[np.arange(R) % 128 // 16]] = e4
    e5 = dgt * gt * (1.0 - gt) * f64(steep)
    s5 = np.zeros((R, J))
    s5[np.arange(R)[:, None], idx2[np.arange(R) % 128 // 16]] = e5
    dh1 = s1 + s2 + s3 + s4 + s5
    da = dh1 * f64(gain)
    hda = da * 2.0
    hdh1 = hda * f64(gain)
    he5 = pick8(hdh1, idx2, 16)
    he4 = pick8(hdh1, idx2, 16)
    he3 = pick8(hdh1, idx3, 16)
    he2 = pick8(hdh1, idx3, 16)
    hdgt = he5 * f64(steep) * (1.0 - gt) * gt + he3 * (-1.0) * f64(steep) * (1.0 - gt) * gt
    hgt = he5 * f64(steep) * (1.0 - gt) * dgt + he4 * c0 + he3 * (-1.0) * f64(steep) * (1.0 - gt) * dgt + he2 * (-1.0) * c0 - he5 * f64(steep) * dgt * gt - he3 * (-1.0) * f64(steep) * dgt * gt
    e51 = hdgt * c0
    s51 = np.zeros((R, J))
    s51[np.arange(R)[:, None], idx2[np.arange(R) % 128 // 16]] = e51
    e52 = hgt * gt * (1.0 - gt) * f64(steep)
    s52 = np.zeros((R, J))
    s52[np.arange(R)[:, None], idx2[np.arange(R) % 128 // 16]] = e52
    e53 = hdgt * c0 * (-1.0)
    s53 = np.zeros((R, J))
    s53[np.arange(R)[:, None], idx3[np.arange(R) % 128 // 16]] = e53
    e54 = hgt * gt * (1.0 - gt) * f64(steep) * (-1.0)
    s54 = np.zeros((R, J))
    s54[np.arange(R)[:, None], idx3[np.arange(R) % 128 // 16]] = e54
    hh1 = s51 + s52 + s53 + s54
    ha = hh1 * f64(gain)
    y = ha * f64(og) + f64(base)
    return y

@@ -1,0 +1,175 @@
+from contextlib import ExitStack
+
+import concourse.mybir as mybir
+
+K, R, F, T, J, M = 512, 128, 512, 2048, 512, 256
+FLOPS = 2 * K * R * J + 2 * F * R * M
+
+F32 = mybir.dt.float32
+BF16 = mybir.dt.bfloat16
+I32 = mybir.dt.int32
+U32 = mybir.dt.uint32
+U16 = mybir.dt.uint16
+U8 = mybir.dt.uint8
+FP8X4 = mybir.dt.float8_e4m3fn_x4
+ALU = mybir.AluOpType
+ACT = mybir.ActivationFunctionType
+
+P = 128
+PACK = 4
+HALVES = 2
+JH = J // HALVES
+MH = M // HALVES
+
+
+def tile_attend_gpcsoftlarger_kernel(tc, tab_words, tab_scales, w1, gain, steep, wo, dy, og, base, offs, offs2, offs3, out):
+    nc = tc.nc
+    with ExitStack() as ctx:
+        lists = ctx.enter_context(tc.tile_pool(name="lists", bufs=1))
+        sb = ctx.enter_context(tc.tile_pool(name="sb", bufs=1))
+        psum = ctx.enter_context(tc.psum_pool(name="psum", bufs=1))
+
+        def new(name, cols, dtype=F32, tag=None):
+            return sb.tile([P, cols], dtype, name=name, tag=tag or name, align_bytes=64)
+
+        def interleave(copy, name, raw, c0, cols):
+            grouped = new(name, cols * PACK, BF16)
+            src = raw[:].rearrange("p (t w) -> p t w", t=PACK)[:, :, c0 : c0 + cols]
+            copy(
+                out=grouped[:].rearrange("p (c i t) -> p c t i", i=4, t=PACK),
+                in_=src.rearrange("p t (c i) -> p c t i", i=4),
+            )
+            return grouped
+
+        def quantise(name, grouped, cols):
+            codes = new(name + "_codes", cols, U32)
+            scales = new(name + "_scales", cols, U8)
+            nc.vector.quantize_mx(out=codes[:].bitcast(FP8X4), scales=scales[:], in_=grouped[:])
+            return codes, scales
+
+        list1 = lists.tile([P, J // 16], U16, name="list1")
+        list2 = lists.tile([P, M // 16], U16, name="list2")
+        list3 = lists.tile([P, M // 16], U16, name="list3")
+        table_scales = new("table_scales", T, U8)
+        nc.vector.memset(table_scales[:].bitcast(I32), 0)
+        nc.sync.dma_start(list1[:], offs)
+        nc.sync.dma_start(list3[:], offs3)
+        w1_raw = sb.tile([P, PACK * R], F32, name="w1_raw", tag="raw_a", align_bytes=64)
+        nc.sync.dma_start(w1_raw[:], w1.rearrange("(p t) r -> p (t r)", t=PACK))
+        wo_raw = sb.tile([P, PACK * R], F32, name="wo_raw", tag="raw_b", align_bytes=64)
+        nc.sync.dma_start(wo_raw[:], wo.rearrange("(p t) r -> p (t r)", t=PACK))
+        for q in range(4):
+            nc.scalar.dma_start(
+                table_scales[32 * q : 32 * q + 4, :].bitcast(I32),
+                tab_scales[0, 4 * q : 4 * q + 4, :].bitcast(I32),
+            )
+        table_words = new("table_words", T, U32)
+        nc.sync.dma_start(table_words[:].bitcast(I32), tab_words[0].rearrange("p c t -> p (c t)").bitcast(I32))
+        gain_col, steep_col, og_col = new("gain_col", 1), new("steep_col", 1), new("og_col", 1)
+        nc.gpsimd.dma_start(gain_col[:], gain)
+        nc.gpsimd.dma_start(steep_col[:], steep)
+        nc.gpsimd.dma_start(og_col[:], og)
+        nc.sync.dma_start(list2[:], offs2)
+
+        warm = new("warm", 1)
+        warm_out = new("warm_out", 1)
+        nc.vector.memset(warm[:], 0.0)
+        nc.scalar.activation(warm_out[:], warm[:], ACT.Silu)
+
+        by2, by3 = new("by2", J), new("by3", J)
+        nc.vector.memset(by2[:], 0.0)
+        nc.vector.memset(by3[:], 0.0)
+
+        w1_codes, w1_scales = quantise("w1", interleave(nc.vector.tensor_copy, "w1_grouped", w1_raw, 0, R), R)
+        wo_codes, wo_scales = quantise("wo", interleave(nc.vector.tensor_copy, "wo_grouped", wo_raw, 0, R), R)
+
+        dy_raw = sb.tile([P, PACK * M], F32, name="dy_raw", tag="raw_a", align_bytes=64)
+        nc.sync.dma_start(dy_raw[:], dy.rearrange("(p t) m -> p (t m)", t=PACK))
+        base_sb = sb.tile([P, J], F32, name="base_sb", tag="raw_b", align_bytes=64)
+        nc.sync.dma_start(base_sb[:], base)
+
+        neg_steep, half_steep, gain_sq, outer = new("neg_steep", 1), new("half_steep", 1), new("gain_sq", 1), new("outer", 1)
+        nc.gpsimd.tensor_tensor(gain_sq[:], gain_col[:], gain_col[:], ALU.mult)
+        nc.gpsimd.tensor_scalar(neg_steep[:], steep_col[:], -1.0, 0.0, ALU.mult, ALU.add)
+        nc.gpsimd.tensor_scalar(half_steep[:], steep_col[:], 0.5, 0.0, ALU.mult, ALU.add)
+        nc.gpsimd.tensor_scalar(outer[:], gain_col[:], og_col[:], half_steep[:], ALU.mult, ALU.mult)
+
+        picked_scales = new("picked_scales", J, U8)
+        nc.vector.tensor_copy(picked_scales[:], table_scales[:].indirect(list1[:]))
+        h1 = new("h1", J)
+        for h in range(HALVES):
+            cols = slice(h * JH, (h + 1) * JH)
+            picked_words = new(f"picked_words{h}", JH, U32)
+            nc.vector.tensor_copy(picked_words[:], table_words[:].indirect(list1[:, h * JH // 16 : (h + 1) * JH // 16]))
+            a = psum.tile([P, JH], F32, name=f"a{h}")
+            nc.tensor.matmul_mx(
+                out=a[:], lhsT=w1_codes[:].bitcast(FP8X4), lhsT_scale=w1_scales[:],
+                rhs=picked_words[:].bitcast(FP8X4), rhs_scale=picked_scales[:, cols], start=True, stop=True,
+            )
+            nc.vector.tensor_scalar(h1[:, cols], a[:], gain_col[:], None, ALU.mult)
+
+        c_first, c_second = [], []
+        for h in range(HALVES):
+            dy_codes, dy_scales = quantise(f"dy{h}", interleave(nc.scalar.copy, f"dy_grouped{h}", dy_raw, h * MH, MH), MH)
+            c0 = psum.tile([P, MH], F32, name=f"c0_{h}")
+            nc.tensor.matmul_mx(
+                out=c0[:], lhsT=wo_codes[:].bitcast(FP8X4), lhsT_scale=wo_scales[:],
+                rhs=dy_codes[:].bitcast(FP8X4), rhs_scale=dy_scales[:], start=True, stop=True,
+            )
+            c_first.append(new(f"c_first{h}", MH))
+            c_second.append(new(f"c_second{h}", MH))
+            nc.scalar.activation(c_first[h][:], c0[:], ACT.Copy, scale=gain_sq[:])
+            nc.scalar.activation(c_second[h][:], c0[:], ACT.Copy, scale=outer[:])
+
+        picks2 = [list2[:, h * MH // 16 : (h + 1) * MH // 16] for h in range(HALVES)]
+        picks3 = [list3[:, h * MH // 16 : (h + 1) * MH // 16] for h in range(HALVES)]
+
+        def difference(name, window, third_tags, diff_tags):
+            third = [new(f"{name}_third{h}", MH, tag=third_tags[h]) for h in range(HALVES)]
+            diff = [new(f"{name}_diff{h}", MH, tag=diff_tags[h]) for h in range(HALVES)]
+            for h in range(HALVES):
+                nc.vector.tensor_copy(third[h][:], window[:].indirect(picks3[h]))
+            for h in range(HALVES):
+                nc.vector.tensor_tensor(diff[h][:], window[:].indirect(picks2[h]), third[h][:], ALU.subtract)
+            return diff
+
+        d = difference("h1", h1, (None, "dy_grouped0"), (None, "dy_grouped1"))
+        t, w2, w3 = [], [], []
+        for h in range(HALVES):
+            y, ym = new(f"y{h}", MH, tag=("raw_a", None)[h]), new(f"ym{h}", MH)
+            t.append(new(f"t{h}", MH))
+            w2.append(new(f"w2_{h}", MH))
+            w3.append(new(f"w3_{h}", MH))
+            nc.scalar.activation(y[:], d[h][:], ACT.Silu, scale=neg_steep[:])
+            nc.scalar.activation(t[h][:], d[h][:], ACT.Tanh, scale=half_steep[:])
+            nc.scalar.activation(ym[:], y[:], ACT.Copy, bias=-1.0)
+            nc.vector.scalar_tensor_tensor(w2[h][:], t[h][:], 1.0, ym[:], ALU.add, ALU.mult)
+            nc.scalar.activation(w3[h][:], w2[h][:], ACT.Copy, bias=2.0)
+        for h in range(HALVES):
+            nc.vector.tensor_tensor(by2[:].indirect(picks2[h]), w2[h][:], c_first[h][:], ALU.mult)
+            nc.vector.tensor_tensor(by3[:].indirect(picks3[h]), w3[h][:], c_first[h][:], ALU.mult)
+
+        curve, factor = [], []
+        for h in range(HALVES):
+            curve.append(new(f"curve{h}", MH))
+            nc.vector.scalar_tensor_tensor(curve[h][:], w2[h][:], 1.0, t[h][:], ALU.add, ALU.mult)
+        hdh1 = new("hdh1", J)
+        nc.vector.tensor_tensor(hdh1[:], by3[:], by2[:], ALU.subtract)
+        for h in range(HALVES):
+            factor.append(new(f"factor{h}", MH))
+            nc.vector.scalar_tensor_tensor(factor[h][:], curve[h][:], 1.0, c_second[h][:], ALU.add, ALU.mult)
+
+        dd = difference("hdh1", hdh1, (None, None), (None, None))
+        for h in range(HALVES):
+            nc.vector.tensor_tensor(by2[:].indirect(picks2[h]), dd[h][:], factor[h][:], ALU.mult)
+            nc.vector.tensor_tensor(by3[:].indirect(picks3[h]), dd[h][:], factor[h][:], ALU.mult)
+
+        partial = [new(f"partial{h}", JH) for h in range(HALVES)]
+        result = [new(f"result{h}", JH) for h in range(HALVES)]
+        for h in range(HALVES):
+            cols = slice(h * JH, (h + 1) * JH)
+            nc.vector.tensor_tensor(partial[h][:], by2[:, cols], base_sb[:, cols], ALU.add)
+        for h, queue in enumerate((nc.sync, nc.scalar)):
+            cols = slice(h * JH, (h + 1) * JH)
+            nc.vector.tensor_tensor(result[h][:], partial[h][:], by3[:, cols], ALU.subtract)
+            queue.dma_start(out[:, cols], result[h][:])

@@ -20,6 +20,7 @@ PACK = 4
 HALVES = 2
 JH = J // HALVES
 MH = M // HALVES
+LAST = 192
 
 
 def tile_attend_gpcsoftlarger_kernel(tc, tab_words, tab_scales, w1, gain, steep, wo, dy, og, base, offs, offs2, offs3, out):
@@ -53,23 +54,27 @@ def tile_attend_gpcsoftlarger_kernel(tc, tab_words, tab_scales, w1, gain, steep,
         table_scales = new("table_scales", T, U8)
         nc.vector.memset(table_scales[:].bitcast(I32), 0)
         nc.sync.dma_start(list1[:], offs)
-        nc.sync.dma_start(list3[:], offs3)
-        w1_raw = sb.tile([P, PACK * R], F32, name="w1_raw", tag="raw_a", align_bytes=64)
+        w1_raw = new("w1_raw", PACK * R)
         nc.sync.dma_start(w1_raw[:], w1.rearrange("(p t) r -> p (t r)", t=PACK))
-        wo_raw = sb.tile([P, PACK * R], F32, name="wo_raw", tag="raw_b", align_bytes=64)
-        nc.sync.dma_start(wo_raw[:], wo.rearrange("(p t) r -> p (t r)", t=PACK))
         for q in range(4):
-            nc.scalar.dma_start(
+            (nc.sync, nc.scalar)[q % 2].dma_start(
                 table_scales[32 * q : 32 * q + 4, :].bitcast(I32),
                 tab_scales[0, 4 * q : 4 * q + 4, :].bitcast(I32),
             )
         table_words = new("table_words", T, U32)
         nc.sync.dma_start(table_words[:].bitcast(I32), tab_words[0].rearrange("p c t -> p (c t)").bitcast(I32))
         gain_col, steep_col, og_col = new("gain_col", 1), new("steep_col", 1), new("og_col", 1)
-        nc.gpsimd.dma_start(gain_col[:], gain)
-        nc.gpsimd.dma_start(steep_col[:], steep)
-        nc.gpsimd.dma_start(og_col[:], og)
+        nc.sync.dma_start(gain_col[:], gain)
+        nc.sync.dma_start(steep_col[:], steep)
+        nc.sync.dma_start(og_col[:], og)
+        wo_raw = new("wo_raw", PACK * R)
+        nc.sync.dma_start(wo_raw[:], wo.rearrange("(p t) r -> p (t r)", t=PACK))
+        dy_raw = new("dy_raw", PACK * M)
+        nc.sync.dma_start(dy_raw[:], dy.rearrange("(p t) m -> p (t m)", t=PACK))
+        nc.sync.dma_start(list3[:], offs3)
         nc.sync.dma_start(list2[:], offs2)
+        base_sb = new("base_sb", J)
+        nc.sync.dma_start(base_sb[:], base)
 
         warm = new("warm", 1)
         warm_out = new("warm_out", 1)
@@ -81,18 +86,15 @@ def tile_attend_gpcsoftlarger_kernel(tc, tab_words, tab_scales, w1, gain, steep,
         nc.vector.memset(by3[:], 0.0)
 
         w1_codes, w1_scales = quantise("w1", interleave(nc.vector.tensor_copy, "w1_grouped", w1_raw, 0, R), R)
-        wo_codes, wo_scales = quantise("wo", interleave(nc.vector.tensor_copy, "wo_grouped", wo_raw, 0, R), R)
-
-        dy_raw = sb.tile([P, PACK * M], F32, name="dy_raw", tag="raw_a", align_bytes=64)
-        nc.sync.dma_start(dy_raw[:], dy.rearrange("(p t) m -> p (t m)", t=PACK))
-        base_sb = sb.tile([P, J], F32, name="base_sb", tag="raw_b", align_bytes=64)
-        nc.sync.dma_start(base_sb[:], base)
+        wo_codes, wo_scales = quantise("wo", interleave(nc.scalar.copy, "wo_grouped", wo_raw, 0, R), R)
 
         neg_steep, half_steep, gain_sq, outer = new("neg_steep", 1), new("half_steep", 1), new("gain_sq", 1), new("outer", 1)
-        nc.gpsimd.tensor_tensor(gain_sq[:], gain_col[:], gain_col[:], ALU.mult)
-        nc.gpsimd.tensor_scalar(neg_steep[:], steep_col[:], -1.0, 0.0, ALU.mult, ALU.add)
-        nc.gpsimd.tensor_scalar(half_steep[:], steep_col[:], 0.5, 0.0, ALU.mult, ALU.add)
-        nc.gpsimd.tensor_scalar(outer[:], gain_col[:], og_col[:], half_steep[:], ALU.mult, ALU.mult)
+        gain_og = new("gain_og", 1)
+        nc.scalar.activation(gain_sq[:], gain_col[:], ACT.Square)
+        nc.scalar.activation(neg_steep[:], steep_col[:], ACT.Copy, scale=-1.0)
+        nc.scalar.activation(half_steep[:], steep_col[:], ACT.Copy, scale=0.5)
+        nc.scalar.activation(gain_og[:], gain_col[:], ACT.Copy, scale=og_col[:])
+        nc.scalar.activation(outer[:], gain_og[:], ACT.Copy, scale=half_steep[:])
 
         picked_scales = new("picked_scales", J, U8)
         nc.vector.tensor_copy(picked_scales[:], table_scales[:].indirect(list1[:]))
@@ -108,24 +110,20 @@ def tile_attend_gpcsoftlarger_kernel(tc, tab_words, tab_scales, w1, gain, steep,
             )
             nc.vector.tensor_scalar(h1[:, cols], a[:], gain_col[:], None, ALU.mult)
 
-        c_first, c_second = [], []
+        c0 = []
         for h in range(HALVES):
             dy_codes, dy_scales = quantise(f"dy{h}", interleave(nc.scalar.copy, f"dy_grouped{h}", dy_raw, h * MH, MH), MH)
-            c0 = psum.tile([P, MH], F32, name=f"c0_{h}")
+            c0.append(psum.tile([P, MH], F32, name=f"c0_{h}"))
             nc.tensor.matmul_mx(
-                out=c0[:], lhsT=wo_codes[:].bitcast(FP8X4), lhsT_scale=wo_scales[:],
+                out=c0[h][:], lhsT=wo_codes[:].bitcast(FP8X4), lhsT_scale=wo_scales[:],
                 rhs=dy_codes[:].bitcast(FP8X4), rhs_scale=dy_scales[:], start=True, stop=True,
             )
-            c_first.append(new(f"c_first{h}", MH))
-            c_second.append(new(f"c_second{h}", MH))
-            nc.scalar.activation(c_first[h][:], c0[:], ACT.Copy, scale=gain_sq[:])
-            nc.scalar.activation(c_second[h][:], c0[:], ACT.Copy, scale=outer[:])
 
         picks2 = [list2[:, h * MH // 16 : (h + 1) * MH // 16] for h in range(HALVES)]
         picks3 = [list3[:, h * MH // 16 : (h + 1) * MH // 16] for h in range(HALVES)]
 
-        def difference(name, window, third_tags, diff_tags):
-            third = [new(f"{name}_third{h}", MH, tag=third_tags[h]) for h in range(HALVES)]
+        def difference(name, window, diff_tags):
+            third = [new(f"{name}_third{h}", MH) for h in range(HALVES)]
             diff = [new(f"{name}_diff{h}", MH, tag=diff_tags[h]) for h in range(HALVES)]
             for h in range(HALVES):
                 nc.vector.tensor_copy(third[h][:], window[:].indirect(picks3[h]))
@@ -133,21 +131,30 @@ def tile_attend_gpcsoftlarger_kernel(tc, tab_words, tab_scales, w1, gain, steep,
                 nc.vector.tensor_tensor(diff[h][:], window[:].indirect(picks2[h]), third[h][:], ALU.subtract)
             return diff
 
-        d = difference("h1", h1, (None, "dy_grouped0"), (None, "dy_grouped1"))
-        t, w2, w3 = [], [], []
+        d = difference("h1", h1, (None, "dy_grouped0"))
+        ym = [new(f"ym{h}", MH) for h in range(HALVES)]
+        w2 = [new(f"w2_{h}", MH) for h in range(HALVES)]
+        w3 = [new(f"w3_{h}", MH) for h in range(HALVES)]
+        c_first, c_second = [], []
+        first_pair = new("first_pair", 2 * MH, tag="dy_raw")
+        y0 = first_pair[:, :MH]
+        t = [first_pair[:, MH:], y0]
+        nc.scalar.activation(y0[:], d[0][:], ACT.Silu, scale=neg_steep[:])
+        nc.scalar.activation(t[0][:], d[0][:], ACT.Tanh, scale=half_steep[:])
+        nc.scalar.activation(ym[0][:], y0[:], ACT.Copy, bias=-1.0)
+        nc.scalar.activation(t[1][:], d[1][:], ACT.Tanh, scale=half_steep[:])
+        nc.scalar.activation(d[1][:], d[1][:], ACT.Silu, scale=neg_steep[:])
+        nc.scalar.activation(ym[1][:], d[1][:], ACT.Copy, bias=-1.0)
         for h in range(HALVES):
-            y, ym = new(f"y{h}", MH, tag=("raw_a", None)[h]), new(f"ym{h}", MH)
-            t.append(new(f"t{h}", MH))
-            w2.append(new(f"w2_{h}", MH))
-            w3.append(new(f"w3_{h}", MH))
-            nc.scalar.activation(y[:], d[h][:], ACT.Silu, scale=neg_steep[:])
-            nc.scalar.activation(t[h][:], d[h][:], ACT.Tanh, scale=half_steep[:])
-            nc.scalar.activation(ym[:], y[:], ACT.Copy, bias=-1.0)
-            nc.vector.scalar_tensor_tensor(w2[h][:], t[h][:], 1.0, ym[:], ALU.add, ALU.mult)
+            nc.vector.scalar_tensor_tensor(w2[h][:], t[h][:], 1.0, ym[h][:], ALU.add, ALU.mult)
+            c_first.append(new(f"c_first{h}", MH, tag=("h1_diff0", "dy_grouped0")[h]))
+            nc.scalar.activation(c_first[h][:], c0[h][:], ACT.Copy, scale=gain_sq[:])
             nc.scalar.activation(w3[h][:], w2[h][:], ACT.Copy, bias=2.0)
-        for h in range(HALVES):
             nc.vector.tensor_tensor(by2[:].indirect(picks2[h]), w2[h][:], c_first[h][:], ALU.mult)
             nc.vector.tensor_tensor(by3[:].indirect(picks3[h]), w3[h][:], c_first[h][:], ALU.mult)
+        for h in range(HALVES):
+            c_second.append(new(f"c_second{h}", MH, tag=f"ym{h}"))
+            nc.scalar.activation(c_second[h][:], c0[h][:], ACT.Copy, scale=outer[:])
 
         curve, factor = [], []
         for h in range(HALVES):
@@ -159,17 +166,16 @@ def tile_attend_gpcsoftlarger_kernel(tc, tab_words, tab_scales, w1, gain, steep,
             factor.append(new(f"factor{h}", MH))
             nc.vector.scalar_tensor_tensor(factor[h][:], curve[h][:], 1.0, c_second[h][:], ALU.add, ALU.mult)
 
-        dd = difference("hdh1", hdh1, (None, None), (None, None))
+        dd = difference("hdh1", hdh1, (None, None))
         for h in range(HALVES):
             nc.vector.tensor_tensor(by2[:].indirect(picks2[h]), dd[h][:], factor[h][:], ALU.mult)
             nc.vector.tensor_tensor(by3[:].indirect(picks3[h]), dd[h][:], factor[h][:], ALU.mult)
 
-        partial = [new(f"partial{h}", JH) for h in range(HALVES)]
-        result = [new(f"result{h}", JH) for h in range(HALVES)]
-        for h in range(HALVES):
-            cols = slice(h * JH, (h + 1) * JH)
+        pieces = (slice(0, J - LAST), slice(J - LAST, J))
+        partial = [new(f"partial{h}", cols.stop - cols.start) for h, cols in enumerate(pieces)]
+        result = [new(f"result{h}", cols.stop - cols.start) for h, cols in enumerate(pieces)]
+        for h, cols in enumerate(pieces):
             nc.vector.tensor_tensor(partial[h][:], by2[:, cols], base_sb[:, cols], ALU.add)
-        for h, queue in enumerate((nc.sync, nc.scalar)):
-            cols = slice(h * JH, (h + 1) * JH)
+        for h, (cols, queue) in enumerate(zip(pieces, (nc.sync, nc.scalar))):
             nc.vector.tensor_tensor(result[h][:], partial[h][:], by3[:, cols], ALU.subtract)
             queue.dma_start(out[:, cols], result[h][:])

@@ -20,7 +20,7 @@ PACK = 4
 HALVES = 2
 JH = J // HALVES
 MH = M // HALVES
-LAST = 192
+LAST = 256
 
 
 def tile_attend_gpcsoftlarger_kernel(tc, tab_words, tab_scales, w1, gain, steep, wo, dy, og, base, offs, offs2, offs3, out):
@@ -42,8 +42,7 @@ def tile_attend_gpcsoftlarger_kernel(tc, tab_words, tab_scales, w1, gain, steep,
             )
             return grouped
 
-        def quantise(name, grouped, cols):
-            codes = new(name + "_codes", cols, U32)
+        def quantise(name, grouped, codes, cols):
             scales = new(name + "_scales", cols, U8)
             nc.vector.quantize_mx(out=codes[:].bitcast(FP8X4), scales=scales[:], in_=grouped[:])
             return codes, scales
@@ -85,8 +84,8 @@ def tile_attend_gpcsoftlarger_kernel(tc, tab_words, tab_scales, w1, gain, steep,
         nc.vector.memset(by2[:], 0.0)
         nc.vector.memset(by3[:], 0.0)
 
-        w1_codes, w1_scales = quantise("w1", interleave(nc.vector.tensor_copy, "w1_grouped", w1_raw, 0, R), R)
-        wo_codes, wo_scales = quantise("wo", interleave(nc.scalar.copy, "wo_grouped", wo_raw, 0, R), R)
+        w1_codes, w1_scales = quantise("w1", interleave(nc.vector.tensor_copy, "w1_grouped", w1_raw, 0, R), new("w1_codes", R, U32), R)
+        wo_codes, wo_scales = quantise("wo", interleave(nc.scalar.copy, "wo_grouped", wo_raw, 0, R), new("wo_codes", R, U32), R)
 
         neg_steep, half_steep, gain_sq, outer = new("neg_steep", 1), new("half_steep", 1), new("gain_sq", 1), new("outer", 1)
         gain_og = new("gain_og", 1)
@@ -110,66 +109,63 @@ def tile_attend_gpcsoftlarger_kernel(tc, tab_words, tab_scales, w1, gain, steep,
             )
             nc.vector.tensor_scalar(h1[:, cols], a[:], gain_col[:], None, ALU.mult)
 
-        c0 = []
-        for h in range(HALVES):
-            dy_codes, dy_scales = quantise(f"dy{h}", interleave(nc.scalar.copy, f"dy_grouped{h}", dy_raw, h * MH, MH), MH)
-            c0.append(psum.tile([P, MH], F32, name=f"c0_{h}"))
+        halves = [slice(h * MH, (h + 1) * MH) for h in range(HALVES)]
+        dy_grouped = [interleave(nc.scalar.copy, f"dy_grouped{h}", dy_raw, h * MH, MH) for h in range(HALVES)]
+
+        def last_layer(h, codes):
+            dy_codes, dy_scales = quantise(f"dy{h}", dy_grouped[h], codes, MH)
+            c0 = psum.tile([P, MH], F32, name=f"c0_{h}")
             nc.tensor.matmul_mx(
-                out=c0[h][:], lhsT=wo_codes[:].bitcast(FP8X4), lhsT_scale=wo_scales[:],
+                out=c0[:], lhsT=wo_codes[:].bitcast(FP8X4), lhsT_scale=wo_scales[:],
                 rhs=dy_codes[:].bitcast(FP8X4), rhs_scale=dy_scales[:], start=True, stop=True,
             )
+            return c0
 
         picks2 = [list2[:, h * MH // 16 : (h + 1) * MH // 16] for h in range(HALVES)]
         picks3 = [list3[:, h * MH // 16 : (h + 1) * MH // 16] for h in range(HALVES)]
 
-        def difference(name, window, diff_tags):
-            third = [new(f"{name}_third{h}", MH) for h in range(HALVES)]
-            diff = [new(f"{name}_diff{h}", MH, tag=diff_tags[h]) for h in range(HALVES)]
-            for h in range(HALVES):
-                nc.vector.tensor_copy(third[h][:], window[:].indirect(picks3[h]))
-            for h in range(HALVES):
-                nc.vector.tensor_tensor(diff[h][:], window[:].indirect(picks2[h]), third[h][:], ALU.subtract)
+        def difference(name, window):
+            by_list3 = new(f"{name}_by_list3", M)
+            diff = [new(f"{name}_diff{h}", MH) for h in range(HALVES)]
+            for h, cols in enumerate(halves):
+                nc.vector.tensor_copy(by_list3[:, cols], window[:].indirect(picks3[h]))
+            for h, cols in enumerate(halves):
+                nc.vector.tensor_tensor(diff[h][:], window[:].indirect(picks2[h]), by_list3[:, cols], ALU.subtract)
             return diff
 
-        d = difference("h1", h1, (None, "dy_grouped0"))
-        ym = [new(f"ym{h}", MH) for h in range(HALVES)]
-        w2 = [new(f"w2_{h}", MH) for h in range(HALVES)]
-        w3 = [new(f"w3_{h}", MH) for h in range(HALVES)]
-        c_first, c_second = [], []
-        first_pair = new("first_pair", 2 * MH, tag="dy_raw")
-        y0 = first_pair[:, :MH]
-        t = [first_pair[:, MH:], y0]
-        nc.scalar.activation(y0[:], d[0][:], ACT.Silu, scale=neg_steep[:])
-        nc.scalar.activation(t[0][:], d[0][:], ACT.Tanh, scale=half_steep[:])
-        nc.scalar.activation(ym[0][:], y0[:], ACT.Copy, bias=-1.0)
-        nc.scalar.activation(t[1][:], d[1][:], ACT.Tanh, scale=half_steep[:])
-        nc.scalar.activation(d[1][:], d[1][:], ACT.Silu, scale=neg_steep[:])
-        nc.scalar.activation(ym[1][:], d[1][:], ACT.Copy, bias=-1.0)
-        for h in range(HALVES):
-            nc.vector.scalar_tensor_tensor(w2[h][:], t[h][:], 1.0, ym[h][:], ALU.add, ALU.mult)
-            c_first.append(new(f"c_first{h}", MH, tag=("h1_diff0", "dy_grouped0")[h]))
-            nc.scalar.activation(c_first[h][:], c0[h][:], ACT.Copy, scale=gain_sq[:])
-            nc.scalar.activation(w3[h][:], w2[h][:], ACT.Copy, bias=2.0)
-            nc.vector.tensor_tensor(by2[:].indirect(picks2[h]), w2[h][:], c_first[h][:], ALU.mult)
-            nc.vector.tensor_tensor(by3[:].indirect(picks3[h]), w3[h][:], c_first[h][:], ALU.mult)
-        for h in range(HALVES):
-            c_second.append(new(f"c_second{h}", MH, tag=f"ym{h}"))
-            nc.scalar.activation(c_second[h][:], c0[h][:], ACT.Copy, scale=outer[:])
+        c0 = [last_layer(0, new("dy0_codes", MH, U32))]
+        d = difference("h1", h1)
+        gate = new("gate", 2 * M, tag="dy_raw")
+        t, y = gate[:, :M], gate[:, M:]
+        ym, w2, w3 = new("ym", M), new("w2", M), new("w3", M)
+        for h, cols in enumerate(halves):
+            nc.scalar.activation(y[:, cols], d[h][:], ACT.Silu, scale=neg_steep[:])
+            nc.scalar.activation(t[:, cols], d[h][:], ACT.Tanh, scale=half_steep[:])
+            if h == 0:
+                nc.vector.tensor_scalar(ym[:, cols], y[:, cols], -1.0, None, ALU.add)
+                c0.append(last_layer(1, new("dy1_codes", MH, U32, tag="h1_by_list3")))
+            else:
+                nc.scalar.activation(ym[:, cols], y[:, cols], ACT.Copy, bias=-1.0)
+            nc.vector.scalar_tensor_tensor(w2[:, cols], t[:, cols], 1.0, ym[:, cols], ALU.add, ALU.mult)
+            c_first = new(f"c_first{h}", MH, tag=f"h1_diff{h}")
+            nc.scalar.activation(c_first[:], c0[h][:], ACT.Copy, scale=gain_sq[:])
+            nc.scalar.activation(w3[:, cols], w2[:, cols], ACT.Copy, bias=2.0)
+            nc.vector.tensor_tensor(by2[:].indirect(picks2[h]), w2[:, cols], c_first[:], ALU.mult)
+            nc.vector.tensor_tensor(by3[:].indirect(picks3[h]), w3[:, cols], c_first[:], ALU.mult)
+        c_second = new("c_second", M, tag="ym")
+        for h, cols in enumerate(halves):
+            nc.scalar.activation(c_second[:, cols], c0[h][:], ACT.Copy, scale=outer[:])
 
-        curve, factor = [], []
-        for h in range(HALVES):
-            curve.append(new(f"curve{h}", MH))
-            nc.vector.scalar_tensor_tensor(curve[h][:], w2[h][:], 1.0, t[h][:], ALU.add, ALU.mult)
+        nc.vector.scalar_tensor_tensor(w2[:], w2[:], 1.0, t, ALU.add, ALU.mult)
         hdh1 = new("hdh1", J)
         nc.vector.tensor_tensor(hdh1[:], by3[:], by2[:], ALU.subtract)
-        for h in range(HALVES):
-            factor.append(new(f"factor{h}", MH))
-            nc.vector.scalar_tensor_tensor(factor[h][:], curve[h][:], 1.0, c_second[h][:], ALU.add, ALU.mult)
+        factor = new("factor", M)
+        nc.vector.scalar_tensor_tensor(factor[:], w2[:], 1.0, c_second[:], ALU.add, ALU.mult)
 
-        dd = difference("hdh1", hdh1, (None, None))
-        for h in range(HALVES):
-            nc.vector.tensor_tensor(by2[:].indirect(picks2[h]), dd[h][:], factor[h][:], ALU.mult)
-            nc.vector.tensor_tensor(by3[:].indirect(picks3[h]), dd[h][:], factor[h][:], ALU.mult)
+        dd = difference("hdh1", hdh1)
+        for h, cols in enumerate(halves):
+            nc.vector.tensor_tensor(by2[:].indirect(picks2[h]), dd[h][:], factor[:, cols], ALU.mult)
+            nc.vector.tensor_tensor(by3[:].indirect(picks3[h]), dd[h][:], factor[:, cols], ALU.mult)
 
         pieces = (slice(0, J - LAST), slice(J - LAST, J))
         partial = [new(f"partial{h}", cols.stop - cols.start) for h, cols in enumerate(pieces)]

from contextlib import ExitStack

import concourse.mybir as mybir

K, R, F, T, J, M = 512, 128, 512, 2048, 512, 256
FLOPS = 2 * K * R * J + 2 * F * R * M

F32 = mybir.dt.float32
BF16 = mybir.dt.bfloat16
I32 = mybir.dt.int32
U32 = mybir.dt.uint32
U16 = mybir.dt.uint16
U8 = mybir.dt.uint8
FP8X4 = mybir.dt.float8_e4m3fn_x4
ALU = mybir.AluOpType
ACT = mybir.ActivationFunctionType

P = 128
PACK = 4
HALVES = 2
JH = J // HALVES
MH = M // HALVES
LAST = 256


def tile_attend_gpcsoftlarger_kernel(tc, tab_words, tab_scales, w1, gain, steep, wo, dy, og, base, offs, offs2, offs3, out):
    nc = tc.nc
    with ExitStack() as ctx:
        lists = ctx.enter_context(tc.tile_pool(name="lists", bufs=1))
        sb = ctx.enter_context(tc.tile_pool(name="sb", bufs=1))
        psum = ctx.enter_context(tc.psum_pool(name="psum", bufs=1))

        def new(name, cols, dtype=F32, tag=None):
            return sb.tile([P, cols], dtype, name=name, tag=tag or name, align_bytes=64)

        def interleave(copy, name, raw, c0, cols):
            grouped = new(name, cols * PACK, BF16)
            src = raw[:].rearrange("p (t w) -> p t w", t=PACK)[:, :, c0 : c0 + cols]
            copy(
                out=grouped[:].rearrange("p (c i t) -> p c t i", i=4, t=PACK),
                in_=src.rearrange("p t (c i) -> p c t i", i=4),
            )
            return grouped

        def quantise(name, grouped, codes, cols):
            scales = new(name + "_scales", cols, U8)
            nc.vector.quantize_mx(out=codes[:].bitcast(FP8X4), scales=scales[:], in_=grouped[:])
            return codes, scales

        list1 = lists.tile([P, J // 16], U16, name="list1")
        list2 = lists.tile([P, M // 16], U16, name="list2")
        list3 = lists.tile([P, M // 16], U16, name="list3")
        table_scales = new("table_scales", T, U8)
        nc.vector.memset(table_scales[:].bitcast(I32), 0)
        nc.sync.dma_start(list1[:], offs)
        w1_raw = new("w1_raw", PACK * R)
        nc.sync.dma_start(w1_raw[:], w1.rearrange("(p t) r -> p (t r)", t=PACK))
        for q in range(4):
            (nc.sync, nc.scalar)[q % 2].dma_start(
                table_scales[32 * q : 32 * q + 4, :].bitcast(I32),
                tab_scales[0, 4 * q : 4 * q + 4, :].bitcast(I32),
            )
        table_words = new("table_words", T, U32)
        nc.sync.dma_start(table_words[:].bitcast(I32), tab_words[0].rearrange("p c t -> p (c t)").bitcast(I32))
        gain_col, steep_col, og_col = new("gain_col", 1), new("steep_col", 1), new("og_col", 1)
        nc.sync.dma_start(gain_col[:], gain)
        nc.sync.dma_start(steep_col[:], steep)
        nc.sync.dma_start(og_col[:], og)
        wo_raw = new("wo_raw", PACK * R)
        nc.sync.dma_start(wo_raw[:], wo.rearrange("(p t) r -> p (t r)", t=PACK))
        dy_raw = new("dy_raw", PACK * M)
        nc.sync.dma_start(dy_raw[:], dy.rearrange("(p t) m -> p (t m)", t=PACK))
        nc.sync.dma_start(list3[:], offs3)
        nc.sync.dma_start(list2[:], offs2)
        base_sb = new("base_sb", J)
        nc.sync.dma_start(base_sb[:], base)

        warm = new("warm", 1)
        warm_out = new("warm_out", 1)
        nc.vector.memset(warm[:], 0.0)
        nc.scalar.activation(warm_out[:], warm[:], ACT.Silu)

        by2, by3 = new("by2", J), new("by3", J)
        nc.vector.memset(by2[:], 0.0)
        nc.vector.memset(by3[:], 0.0)

        w1_codes, w1_scales = quantise("w1", interleave(nc.vector.tensor_copy, "w1_grouped", w1_raw, 0, R), new("w1_codes", R, U32), R)
        wo_codes, wo_scales = quantise("wo", interleave(nc.scalar.copy, "wo_grouped", wo_raw, 0, R), new("wo_codes", R, U32), R)

        neg_steep, half_steep, gain_sq, outer = new("neg_steep", 1), new("half_steep", 1), new("gain_sq", 1), new("outer", 1)
        gain_og = new("gain_og", 1)
        nc.scalar.activation(gain_sq[:], gain_col[:], ACT.Square)
        nc.scalar.activation(neg_steep[:], steep_col[:], ACT.Copy, scale=-1.0)
        nc.scalar.activation(half_steep[:], steep_col[:], ACT.Copy, scale=0.5)
        nc.scalar.activation(gain_og[:], gain_col[:], ACT.Copy, scale=og_col[:])
        nc.scalar.activation(outer[:], gain_og[:], ACT.Copy, scale=half_steep[:])

        picked_scales = new("picked_scales", J, U8)
        nc.vector.tensor_copy(picked_scales[:], table_scales[:].indirect(list1[:]))
        h1 = new("h1", J)
        for h in range(HALVES):
            cols = slice(h * JH, (h + 1) * JH)
            picked_words = new(f"picked_words{h}", JH, U32)
            nc.vector.tensor_copy(picked_words[:], table_words[:].indirect(list1[:, h * JH // 16 : (h + 1) * JH // 16]))
            a = psum.tile([P, JH], F32, name=f"a{h}")
            nc.tensor.matmul_mx(
                out=a[:], lhsT=w1_codes[:].bitcast(FP8X4), lhsT_scale=w1_scales[:],
                rhs=picked_words[:].bitcast(FP8X4), rhs_scale=picked_scales[:, cols], start=True, stop=True,
            )
            nc.vector.tensor_scalar(h1[:, cols], a[:], gain_col[:], None, ALU.mult)

        halves = [slice(h * MH, (h + 1) * MH) for h in range(HALVES)]
        dy_grouped = [interleave(nc.scalar.copy, f"dy_grouped{h}", dy_raw, h * MH, MH) for h in range(HALVES)]

        def last_layer(h, codes):
            dy_codes, dy_scales = quantise(f"dy{h}", dy_grouped[h], codes, MH)
            c0 = psum.tile([P, MH], F32, name=f"c0_{h}")
            nc.tensor.matmul_mx(
                out=c0[:], lhsT=wo_codes[:].bitcast(FP8X4), lhsT_scale=wo_scales[:],
                rhs=dy_codes[:].bitcast(FP8X4), rhs_scale=dy_scales[:], start=True, stop=True,
            )
            return c0

        picks2 = [list2[:, h * MH // 16 : (h + 1) * MH // 16] for h in range(HALVES)]
        picks3 = [list3[:, h * MH // 16 : (h + 1) * MH // 16] for h in range(HALVES)]

        def difference(name, window):
            by_list3 = new(f"{name}_by_list3", M)
            diff = [new(f"{name}_diff{h}", MH) for h in range(HALVES)]
            for h, cols in enumerate(halves):
                nc.vector.tensor_copy(by_list3[:, cols], window[:].indirect(picks3[h]))
            for h, cols in enumerate(halves):
                nc.vector.tensor_tensor(diff[h][:], window[:].indirect(picks2[h]), by_list3[:, cols], ALU.subtract)
            return diff

        c0 = [last_layer(0, new("dy0_codes", MH, U32))]
        d = difference("h1", h1)
        gate = new("gate", 2 * M, tag="dy_raw")
        t, y = gate[:, :M], gate[:, M:]
        ym, w2, w3 = new("ym", M), new("w2", M), new("w3", M)
        for h, cols in enumerate(halves):
            nc.scalar.activation(y[:, cols], d[h][:], ACT.Silu, scale=neg_steep[:])
            nc.scalar.activation(t[:, cols], d[h][:], ACT.Tanh, scale=half_steep[:])
            if h == 0:
                nc.vector.tensor_scalar(ym[:, cols], y[:, cols], -1.0, None, ALU.add)
                c0.append(last_layer(1, new("dy1_codes", MH, U32, tag="h1_by_list3")))
            else:
                nc.scalar.activation(ym[:, cols], y[:, cols], ACT.Copy, bias=-1.0)
            nc.vector.scalar_tensor_tensor(w2[:, cols], t[:, cols], 1.0, ym[:, cols], ALU.add, ALU.mult)
            c_first = new(f"c_first{h}", MH, tag=f"h1_diff{h}")
            nc.scalar.activation(c_first[:], c0[h][:], ACT.Copy, scale=gain_sq[:])
            nc.scalar.activation(w3[:, cols], w2[:, cols], ACT.Copy, bias=2.0)
            nc.vector.tensor_tensor(by2[:].indirect(picks2[h]), w2[:, cols], c_first[:], ALU.mult)
            nc.vector.tensor_tensor(by3[:].indirect(picks3[h]), w3[:, cols], c_first[:], ALU.mult)
        c_second = new("c_second", M, tag="ym")
        for h, cols in enumerate(halves):
            nc.scalar.activation(c_second[:, cols], c0[h][:], ACT.Copy, scale=outer[:])

        nc.vector.scalar_tensor_tensor(w2[:], w2[:], 1.0, t, ALU.add, ALU.mult)
        hdh1 = new("hdh1", J)
        nc.vector.tensor_tensor(hdh1[:], by3[:], by2[:], ALU.subtract)
        factor = new("factor", M)
        nc.vector.scalar_tensor_tensor(factor[:], w2[:], 1.0, c_second[:], ALU.add, ALU.mult)

        dd = difference("hdh1", hdh1)
        for h, cols in enumerate(halves):
            nc.vector.tensor_tensor(by2[:].indirect(picks2[h]), dd[h][:], factor[:, cols], ALU.mult)
            nc.vector.tensor_tensor(by3[:].indirect(picks3[h]), dd[h][:], factor[:, cols], ALU.mult)

        pieces = (slice(0, J - LAST), slice(J - LAST, J))
        partial = [new(f"partial{h}", cols.stop - cols.start) for h, cols in enumerate(pieces)]
        result = [new(f"result{h}", cols.stop - cols.start) for h, cols in enumerate(pieces)]
        for h, cols in enumerate(pieces):
            nc.vector.tensor_tensor(partial[h][:], by2[:, cols], base_sb[:, cols], ALU.add)
        for h, (cols, queue) in enumerate(zip(pieces, (nc.sync, nc.scalar))):
            nc.vector.tensor_tensor(result[h][:], partial[h][:], by3[:, cols], ALU.subtract)
            queue.dma_start(out[:, cols], result[h][:])
